import numpy as np
import ml_dtypes

BF16 = ml_dtypes.bfloat16


def bf(x):
    return np.asarray(x, np.float32).astype(BF16)


def f32(x):
    return np.asarray(x, np.float32)


def f64(x):
    return np.asarray(x).astype(np.float64)


def striped(idx):
    return np.tile(idx.reshape(-1, 16).T, (8, 1))


S, K, M, N, V, D = 256, 128, 512, 128, 1, 256


def setup_inputs():
    return {"base": bf(np.random.standard_normal((M, S))), "x": bf(np.random.standard_normal((K, N))), "w": bf(1.5 * np.random.standard_normal((K, M)) / np.sqrt(K)), "offs": striped(np.random.permutation(S)[:N])}


def reference(base, x, w, offs):
    idx = offs[:16].T.reshape(-1)
    z = f64(base).copy()
    z[:, idx] += f64(w).T @ f64(x)
    u = z.reshape(M, V, D)
    u = u - u.max(axis=2, keepdims=True)
    u = u - np.log(np.exp(u).sum(axis=2, keepdims=True))
    return u.reshape(M, S)

@@ -1,0 +1,56 @@
+import concourse.mybir as mybir
+from concourse.masks import make_identity
+
+BF16, F32, U16 = mybir.dt.bfloat16, mybir.dt.float32, mybir.dt.uint16
+ADD, SUBTRACT = mybir.AluOpType.add, mybir.AluOpType.subtract
+EXP, LN = mybir.ActivationFunctionType.Exp, mybir.ActivationFunctionType.Ln
+P = 128
+WORDS = 256
+WINDOWS = 4
+
+FLOPS = 2 * P * (WINDOWS * P) * P
+
+
+def tile_rows_rescore_kernel(tc, base, x, w, offs, out):
+    nc = tc.nc
+    with (
+        tc.tile_pool(name="held", bufs=1) as held,
+        tc.psum_pool(name="psum", bufs=1) as psum,
+    ):
+        base_sb = held.tile([P, WINDOWS, WORDS], BF16, name="base_sb")
+        w_sb = held.tile([P, WINDOWS * P], BF16, name="w_sb")
+        x_sb = held.tile([P, P], BF16, name="x_sb")
+        offsets = held.tile([P, P // 16], U16, name="offsets")
+
+        nc.sync.dma_start(base_sb[:], base.rearrange("(a p) s -> p a s", p=P))
+        nc.sync.dma_start(w_sb[:], w)
+        nc.sync.dma_start(x_sb[:], x)
+        nc.sync.dma_start(offsets[:], offs)
+
+        ident = held.tile([P, P], BF16, name="ident")
+        make_identity(nc, ident[:])
+
+        z = [psum.tile([P, WORDS], F32, name=f"z{a}") for a in range(WINDOWS)]
+        for a in range(WINDOWS):
+            nc.tensor.matmul(z[a][:], ident[:], base_sb[:, a, :], start=True, stop=False)
+        for a in range(WINDOWS):
+            nc.tensor.matmul(
+                z[a][:].indirect(offsets[:]), w_sb[:, a * P : (a + 1) * P], x_sb[:], start=False, stop=True
+            )
+
+        neg_max = held.tile([P, WINDOWS], F32, name="neg_max")
+        sums = held.tile([P, WINDOWS], F32, name="sums")
+        log_sums = held.tile([P, WINDOWS], F32, name="log_sums")
+        exps = held.tile([P, WINDOWS, WORDS], BF16, name="exps")
+        result = held.tile([P, WINDOWS, WORDS], F32, name="result")
+        for a in range(WINDOWS):
+            nc.vector.reduce_max(neg_max[:, a : a + 1], z[a][:], mybir.AxisListType.X, negate=True)
+            nc.scalar.activation(
+                exps[:, a, :], z[a][:], EXP, bias=neg_max[:, a : a + 1], accum_out=sums[:, a : a + 1]
+            )
+        nc.scalar.activation(log_sums[:], sums[:], LN)
+        for a in range(WINDOWS):
+            nc.vector.tensor_scalar(
+                result[:, a, :], z[a][:], neg_max[:, a : a + 1], log_sums[:, a : a + 1], ADD, SUBTRACT
+            )
+            nc.sync.dma_start(out[a * P : (a + 1) * P, :], result[:, a, :])

@@ -1,12 +1,22 @@
+import math
+
 import concourse.mybir as mybir
 from concourse.masks import make_identity
 
 BF16, F32, U16 = mybir.dt.bfloat16, mybir.dt.float32, mybir.dt.uint16
-ADD, SUBTRACT = mybir.AluOpType.add, mybir.AluOpType.subtract
-EXP, LN = mybir.ActivationFunctionType.Exp, mybir.ActivationFunctionType.Ln
+I32, U32 = mybir.dt.int32, mybir.dt.uint32
+ADD, SUBTRACT, MULT = mybir.AluOpType.add, mybir.AluOpType.subtract, mybir.AluOpType.mult
+EXP, SQUARE = mybir.ActivationFunctionType.Exp, mybir.ActivationFunctionType.Square
 P = 128
 WORDS = 256
 WINDOWS = 4
+
+BITS_OF_ONE = float(127 << 23)
+LN2_PER_BIT = math.log(2.0) / float(1 << 23)
+K = 1.000225
+ROOT_HALF = math.sqrt(0.5)
+INVERSE_BIAS = round((BITS_OF_ONE * LN2_PER_BIT + math.log(ROOT_HALF) - 0.03) * 512) / 512
+CENTRE = BITS_OF_ONE * LN2_PER_BIT + math.log(ROOT_HALF) - INVERSE_BIAS
 
 FLOPS = 2 * P * (WINDOWS * P) * P
 
@@ -27,6 +37,10 @@ def tile_rows_rescore_kernel(tc, base, x, w, offs, out):
         nc.sync.dma_start(x_sb[:], x)
         nc.sync.dma_start(offsets[:], offs)
 
+        inverse_bias = held.tile([P, 1], F32, name="inverse_bias")
+        square_bias = held.tile([P, 1], F32, name="square_bias")
+        nc.vector.memset(inverse_bias[:], INVERSE_BIAS)
+        nc.vector.memset(square_bias[:], -(1.0 + K) * ROOT_HALF)
         ident = held.tile([P, P], BF16, name="ident")
         make_identity(nc, ident[:])
 
@@ -40,17 +54,25 @@ def tile_rows_rescore_kernel(tc, base, x, w, offs, out):
 
         neg_max = held.tile([P, WINDOWS], F32, name="neg_max")
         sums = held.tile([P, WINDOWS], F32, name="sums")
-        log_sums = held.tile([P, WINDOWS], F32, name="log_sums")
+        guess = held.tile([P, WINDOWS], F32, name="guess")
+        shift = held.tile([P, WINDOWS], F32, name="shift")
+        inverse = held.tile([P, WINDOWS], F32, name="inverse")
+        square = held.tile([P, WINDOWS], F32, name="square")
         exps = held.tile([P, WINDOWS, WORDS], BF16, name="exps")
         result = held.tile([P, WINDOWS, WORDS], F32, name="result")
         for a in range(WINDOWS):
-            nc.vector.reduce_max(neg_max[:, a : a + 1], z[a][:], mybir.AxisListType.X, negate=True)
+            col = slice(a, a + 1)
+            nc.vector.reduce_max(neg_max[:, col], z[a][:], mybir.AxisListType.X, negate=True)
+            nc.scalar.activation(exps[:, a, :], z[a][:], EXP, bias=neg_max[:, col], accum_out=sums[:, col])
             nc.scalar.activation(
-                exps[:, a, :], z[a][:], EXP, bias=neg_max[:, a : a + 1], accum_out=sums[:, a : a + 1]
+                inverse[:, col], sums[:, col].bitcast(U32), EXP, scale=-LN2_PER_BIT, bias=inverse_bias[:]
             )
-        nc.scalar.activation(log_sums[:], sums[:], LN)
-        for a in range(WINDOWS):
+            nc.scalar.activation(square[:, col], inverse[:, col], SQUARE, scale=sums[:, col], bias=square_bias[:])
             nc.vector.tensor_scalar(
-                result[:, a, :], z[a][:], neg_max[:, a : a + 1], log_sums[:, a : a + 1], ADD, SUBTRACT
+                guess[:, col], sums[:, col].bitcast(I32), BITS_OF_ONE, LN2_PER_BIT, SUBTRACT, MULT
             )
+            nc.vector.scalar_tensor_tensor(
+                shift[:, col], neg_max[:, col], -CENTRE - K * K / 2.0, guess[:, col], ADD, SUBTRACT
+            )
+            nc.vector.tensor_scalar(result[:, a, :], z[a][:], shift[:, col], square[:, col], ADD, ADD)
             nc.sync.dma_start(out[a * P : (a + 1) * P, :], result[:, a, :])

@@ -10,6 +10,7 @@ EXP, SQUARE = mybir.ActivationFunctionType.Exp, mybir.ActivationFunctionType.Squ
 P = 128
 WORDS = 256
 WINDOWS = 4
+WARM_UPS = 3
 
 BITS_OF_ONE = float(127 << 23)
 LN2_PER_BIT = math.log(2.0) / float(1 << 23)
@@ -41,8 +42,16 @@ def tile_rows_rescore_kernel(tc, base, x, w, offs, out):
         square_bias = held.tile([P, 1], F32, name="square_bias")
         nc.vector.memset(inverse_bias[:], INVERSE_BIAS)
         nc.vector.memset(square_bias[:], -(1.0 + K) * ROOT_HALF)
+        early = held.tile([P, 1], F32, name="early")
+        nc.scalar.activation(early[:], square_bias[:], EXP)
         ident = held.tile([P, P], BF16, name="ident")
         make_identity(nc, ident[:])
+
+        zeros = held.tile([P, 512], BF16, name="zeros")
+        spare = psum.tile([P, 512], F32, name="spare")
+        nc.vector.memset(zeros[:], 0.0)
+        for turn in range(WARM_UPS):
+            nc.tensor.matmul(spare[:], zeros[:, :P], zeros[:], start=True, stop=True)
 
         z = [psum.tile([P, WORDS], F32, name=f"z{a}") for a in range(WINDOWS)]
         for a in range(WINDOWS):

import math

import concourse.mybir as mybir
from concourse.masks import make_identity

BF16, F32, U16 = mybir.dt.bfloat16, mybir.dt.float32, mybir.dt.uint16
I32, U32 = mybir.dt.int32, mybir.dt.uint32
ADD, SUBTRACT, MULT = mybir.AluOpType.add, mybir.AluOpType.subtract, mybir.AluOpType.mult
EXP, SQUARE = mybir.ActivationFunctionType.Exp, mybir.ActivationFunctionType.Square
P = 128
WORDS = 256
WINDOWS = 4
WARM_UPS = 3

BITS_OF_ONE = float(127 << 23)
LN2_PER_BIT = math.log(2.0) / float(1 << 23)
K = 1.000225
ROOT_HALF = math.sqrt(0.5)
INVERSE_BIAS = round((BITS_OF_ONE * LN2_PER_BIT + math.log(ROOT_HALF) - 0.03) * 512) / 512
CENTRE = BITS_OF_ONE * LN2_PER_BIT + math.log(ROOT_HALF) - INVERSE_BIAS

FLOPS = 2 * P * (WINDOWS * P) * P


def tile_rows_rescore_kernel(tc, base, x, w, offs, out):
    nc = tc.nc
    with (
        tc.tile_pool(name="held", bufs=1) as held,
        tc.psum_pool(name="psum", bufs=1) as psum,
    ):
        base_sb = held.tile([P, WINDOWS, WORDS], BF16, name="base_sb")
        w_sb = held.tile([P, WINDOWS * P], BF16, name="w_sb")
        x_sb = held.tile([P, P], BF16, name="x_sb")
        offsets = held.tile([P, P // 16], U16, name="offsets")

        nc.sync.dma_start(base_sb[:], base.rearrange("(a p) s -> p a s", p=P))
        nc.sync.dma_start(w_sb[:], w)
        nc.sync.dma_start(x_sb[:], x)
        nc.sync.dma_start(offsets[:], offs)

        inverse_bias = held.tile([P, 1], F32, name="inverse_bias")
        square_bias = held.tile([P, 1], F32, name="square_bias")
        nc.vector.memset(inverse_bias[:], INVERSE_BIAS)
        nc.vector.memset(square_bias[:], -(1.0 + K) * ROOT_HALF)
        early = held.tile([P, 1], F32, name="early")
        nc.scalar.activation(early[:], square_bias[:], EXP)
        ident = held.tile([P, P], BF16, name="ident")
        make_identity(nc, ident[:])

        zeros = held.tile([P, 512], BF16, name="zeros")
        spare = psum.tile([P, 512], F32, name="spare")
        nc.vector.memset(zeros[:], 0.0)
        for turn in range(WARM_UPS):
            nc.tensor.matmul(spare[:], zeros[:, :P], zeros[:], start=True, stop=True)

        z = [psum.tile([P, WORDS], F32, name=f"z{a}") for a in range(WINDOWS)]
        for a in range(WINDOWS):
            nc.tensor.matmul(z[a][:], ident[:], base_sb[:, a, :], start=True, stop=False)
        for a in range(WINDOWS):
            nc.tensor.matmul(
                z[a][:].indirect(offsets[:]), w_sb[:, a * P : (a + 1) * P], x_sb[:], start=False, stop=True
            )

        neg_max = held.tile([P, WINDOWS], F32, name="neg_max")
        sums = held.tile([P, WINDOWS], F32, name="sums")
        guess = held.tile([P, WINDOWS], F32, name="guess")
        shift = held.tile([P, WINDOWS], F32, name="shift")
        inverse = held.tile([P, WINDOWS], F32, name="inverse")
        square = held.tile([P, WINDOWS], F32, name="square")
        exps = held.tile([P, WINDOWS, WORDS], BF16, name="exps")
        result = held.tile([P, WINDOWS, WORDS], F32, name="result")
        for a in range(WINDOWS):
            col = slice(a, a + 1)
            nc.vector.reduce_max(neg_max[:, col], z[a][:], mybir.AxisListType.X, negate=True)
            nc.scalar.activation(exps[:, a, :], z[a][:], EXP, bias=neg_max[:, col], accum_out=sums[:, col])
            nc.scalar.activation(
                inverse[:, col], sums[:, col].bitcast(U32), EXP, scale=-LN2_PER_BIT, bias=inverse_bias[:]
            )
            nc.scalar.activation(square[:, col], inverse[:, col], SQUARE, scale=sums[:, col], bias=square_bias[:])
            nc.vector.tensor_scalar(
                guess[:, col], sums[:, col].bitcast(I32), BITS_OF_ONE, LN2_PER_BIT, SUBTRACT, MULT
            )
            nc.vector.scalar_tensor_tensor(
                shift[:, col], neg_max[:, col], -CENTRE - K * K / 2.0, guess[:, col], ADD, SUBTRACT
            )
            nc.vector.tensor_scalar(result[:, a, :], z[a][:], shift[:, col], square[:, col], ADD, ADD)
            nc.sync.dma_start(out[a * P : (a + 1) * P, :], result[:, a, :])
